import numpy as np
import ml_dtypes


def mxq(x, axis, fmt="e4m3"):
    dtype, down = {"e4m3": (ml_dtypes.float8_e4m3fn, 7), "e5m2": (ml_dtypes.float8_e5m2, 14)}[fmt]
    v = np.moveaxis(np.asarray(x, np.float32).astype(ml_dtypes.bfloat16).astype(np.float64), axis, -1)
    blocks = v.reshape(v.shape[:-1] + (-1, 32))
    amax = np.abs(blocks).max(-1, keepdims=True)
    byte = np.maximum(np.where(amax > 0, np.frexp(amax)[1] - 1 + 127, 0) - down, 1)
    scale = np.exp2(byte - 127.0)
    codes = (blocks / scale).astype(np.float32).astype(dtype).astype(np.float64)
    return np.moveaxis((codes * scale).reshape(v.shape), -1, axis)


WIDE = False


def mx_kscale(k):
    if not WIDE:
        return np.ones(k)
    levels = np.array([10, -10, 5, -5, 0])
    if k % 512:
        return np.exp2(np.random.permutation(np.resize(levels, k // 32))).repeat(32)
    a = np.empty((k // 512, 16))
    for p in range(k // 512):
        a[p, :8] = np.random.permutation(np.resize(levels, 8))
        for g in range(8):
            far = levels[np.abs(levels - a[p, g]) >= 10]
            a[p, g + 8] = far[np.random.randint(len(far))]
    return np.exp2(a.ravel()).repeat(32)


def f64(x):
    return np.asarray(x).astype(np.float64)


def striped(idx):
    return np.tile(idx.reshape(-1, 16).T, (8, 1)).astype(np.uint16)


def unstriped(offs):
    return offs[:16].T.reshape(-1).astype(np.int64)


E2M1 = np.array([0.0, 0.5, 1.0, 1.5, 2.0, 3.0, 4.0, 6.0, -0.0, -0.5, -1.0, -1.5, -2.0, -3.0, -4.0, -6.0])


def pack_weight(w, fmt):
    k, n = w.shape
    w = f64(np.asarray(w, np.float32).astype(ml_dtypes.bfloat16)).reshape(k // 32, 32, n)
    amax = np.abs(w).max(1)
    if fmt == "e4m3":
        byte = np.frexp(amax)[1] - 1 + 127 - 7
    else:
        mant, ex = np.frexp(amax / 6.0)
        byte = np.where(mant > 0.5, ex, ex - 1) + 127
    byte = np.clip(np.where(amax > 0, byte, 1), 1, 254)
    scaled = (w * np.exp2(127.0 - byte)[:, None, :]).reshape(k, n).astype(np.float32)
    by_word = np.ascontiguousarray(scaled.reshape(k // 512, 128, 4, n).transpose(0, 1, 3, 2))
    if fmt == "e4m3":
        words = by_word.astype(ml_dtypes.float8_e4m3fn).view(np.uint8)
    else:
        c = by_word.astype(ml_dtypes.float4_e2m1fn).view(np.uint8) & 0xF
        words = (c[..., 0::2] | (c[..., 1::2] << 4)).reshape(k // 512, 128, 2 * n)
    return np.ascontiguousarray(words), np.ascontiguousarray(byte.astype(np.uint8).reshape(k // 512, 16, n))


def unpack_weight(words, scales, fmt):
    g, _, n = scales.shape
    words = np.ascontiguousarray(words).reshape(g, 128, n, -1)
    if fmt == "e4m3":
        vals = words.view(ml_dtypes.float8_e4m3fn).astype(np.float64)
    else:
        nib = np.empty((g, 128, n, 4), np.uint8)
        nib[..., 0::2] = words & 0xF
        nib[..., 1::2] = words >> 4
        vals = E2M1[nib]
    vals = vals * np.repeat(np.exp2(scales.astype(np.float64) - 127.0), 8, axis=1)[..., None]
    return vals.transpose(0, 1, 3, 2).reshape(g * 512, n)


def gelu(v):
    return 0.5 * v * (1.0 + np.tanh(np.sqrt(2.0 / np.pi) * (v + 0.044715 * v**3)))


K, M, H, N, T, S, TF, P = 1024, 512, 1024, 512, 4096, 1024, 2048, 512

def setup_inputs():
    n = np.random.standard_normal
    s, s2, u = mx_kscale(K)[:, None], mx_kscale(M)[:, None], mx_kscale(H)[:, None]
    d = {}
    d["tab_words"], d["tab_scales"] = pack_weight(n((K, T)) * s, "e4m3")
    d["offs"] = striped(np.random.permutation(T)[:S])
    d["tab2_words"], d["tab2_scales"] = pack_weight(n((M, TF)) * s2, "e4m3")
    d["offs2"] = striped(np.random.permutation(TF)[:P])
    d["pos1"] = striped(np.random.permutation(S)[:P])
    d["w1"] = (1.3 * n((K, H)) / K**0.5 / s).astype(np.float32)
    d["gain"] = (u[:, 0] * np.random.choice([-1.0, 1.0], H) * np.random.uniform(0.6, 1.4, H)).astype(np.float32)
    d["w2_words"], d["w2_scales"] = pack_weight(n((M, H)) / M**0.5 / s2 * u.T, "e2m1")
    d["w3"] = (n((M, H)) / M**0.5 / s2).astype(np.float32)
    d["wgs"] = np.exp(0.3 * n((128, P))).astype(np.float32)
    d["gm"] = n((H, S)).astype(np.float32)
    d["w4_words"], d["w4_scales"] = pack_weight(n((H, N)) / H**0.5 / u, "e2m1")
    d["w5"] = (n((H, N)) / H**0.5 / u).astype(np.float32)
    return d

def reference(tab_words, tab_scales, offs, tab2_words, tab2_scales, offs2, pos1, w1, gain, w2_words, w2_scales, w3, wgs, gm, w4_words, w4_scales, w5):
    v = unpack_weight(tab_words, tab_scales, "e4m3")[:, unstriped(offs)]
    v2 = unpack_weight(tab2_words, tab2_scales, "e4m3")[:, unstriped(offs2)]
    a = f64(gain)[:, None] * np.exp(np.tanh(mxq(f64(w1), 0, "e4m3").T @ v))
    b2 = unpack_weight(w2_words, w2_scales, "e2m1").T @ v2
    b3 = mxq(f64(w3), 0, "e4m3").T @ v2
    b = b2 * b3
    placed = np.zeros((H, S))
    placed[:, unstriped(pos1)] = np.tile(f64(wgs), (H // 128, 1)) * b
    z = a - placed
    zg = mxq(z * f64(gm), 0, "e4m3")
    za = mxq(np.abs(z), 0, "e4m3")
    w4 = unpack_weight(w4_words, w4_scales, "e2m1")
    w5q = mxq(f64(w5), 0, "e4m3")
    return w4.T @ zg + w5q.T @ za

@@ -1,0 +1,298 @@
+from contextlib import ExitStack
+
+import concourse.mybir as mybir
+
+K, M, H, N, T, S, TF, PL = 1024, 512, 1024, 512, 4096, 1024, 2048, 512
+FLOPS = 2 * (K * H * S + 2 * M * H * PL + 2 * H * N * S)
+
+F32 = mybir.dt.float32
+BF16 = mybir.dt.bfloat16
+I32 = mybir.dt.int32
+U32 = mybir.dt.uint32
+U16 = mybir.dt.uint16
+U8 = mybir.dt.uint8
+FP8X4 = mybir.dt.float8_e4m3fn_x4
+FP4X4 = mybir.dt.float4_e2m1fn_x4
+ALU = mybir.AluOpType
+ACT = mybir.ActivationFunctionType
+
+P = 128
+PACK = 4
+KP = P * PACK
+BANK = 512
+
+
+def tile_list_crash_injury_scores_kernel(
+    tc, tab_words, tab_scales, offs, tab2_words, tab2_scales, offs2, pos1, w1, gain,
+    w2_words, w2_scales, w3, wgs, gm, w4_words, w4_scales, w5, out,
+):
+    nc = tc.nc
+    groups = H // KP
+    halves = S // BANK
+
+    with ExitStack() as ctx:
+        lists = ctx.enter_context(tc.tile_pool(name="lists", bufs=1))
+        keep = ctx.enter_context(tc.tile_pool(name="keep", bufs=1))
+        ring = ctx.enter_context(tc.tile_pool(name="ring", bufs=1))
+        overlay = ctx.enter_context(tc.tile_pool(name="overlay", bufs=1))
+        late = ctx.enter_context(tc.tile_pool(name="late", bufs=1))
+        psum = ctx.enter_context(tc.psum_pool(name="psum", bufs=1))
+
+        def raw_tile(name, shape, dtype):
+            return ring.tile(shape, dtype, name=name, tag="raw", bufs=3, align_bytes=64)
+
+        def code_tiles(name):
+            words = ring.tile([P, BANK], U32, name=name + "_w", tag="words", bufs=8, align_bytes=64)
+            scales = ring.tile([P, BANK], U8, name=name + "_s", tag="scales", bufs=8, align_bytes=64)
+            return words, scales
+
+        def quantize(name, grouped):
+            words, scales = code_tiles(name)
+            nc.vector.quantize_mx(out=words[:].bitcast(FP8X4), scales=scales[:], in_=grouped)
+            return words, scales
+
+        def load_scale_rows(queue, tile, rows):
+            for q in range(4):
+                queue.dma_start(out=tile(q).bitcast(I32), in_=rows(q).bitcast(I32))
+
+        t2s = keep.tile([P, TF], U8, name="t2s", align_bytes=64)
+        w2s_raw = keep.tile([P, H], U8, name="w2s_raw", align_bytes=64)
+        t1s = keep.tile([P, T], U8, name="t1s", align_bytes=64)
+        w4s = keep.tile([P, groups, N], U8, name="w4s", align_bytes=64)
+        nc.gpsimd.memset(t2s[:].bitcast(I32), 0)
+        nc.gpsimd.memset(w2s_raw[:].bitcast(I32), 0)
+        nc.vector.memset(t1s[:].bitcast(I32), 0)
+        nc.gpsimd.memset(w4s[:].rearrange("p a n -> p (a n)").bitcast(I32), 0)
+        pages = [keep.tile([P, S], F32, name="page%d" % i) for i in range(PACK)]
+        for i in range(PACK):
+            nc.vector.memset(pages[i][:], 0.0)
+
+        def load_weight(raw, w, a, cols):
+            nc.sync.dma_start(out=raw[:], in_=w[a * KP : (a + 1) * KP, cols].rearrange("(p j) c -> p j c", j=PACK))
+            return raw
+
+        def ring_raw(name):
+            return raw_tile(name, [P, PACK, BANK], F32)
+
+        def group_cols(b):
+            return slice(b * KP, (b + 1) * KP)
+
+        offs2_t = lists.tile([P, PL // 16], U16, name="offs2_t")
+        nc.sync.dma_start(offs2_t[:], offs2)
+        w2w_raw = keep.tile([P, 2 * H], U8, name="w2w_raw", align_bytes=64)
+        nc.sync.dma_start(out=w2w_raw[:].bitcast(I32), in_=w2_words[0].bitcast(I32))
+        first_raw = overlay.tile([P, PACK, BANK], F32, name="w3_raw0", offset=0, align_bytes=64)
+        w3_raw = [load_weight(first_raw, w3, 0, group_cols(0))]
+        load_scale_rows(nc.sync, lambda q: t2s[32 * q : 32 * q + 4, :], lambda q: tab2_scales[0, 4 * q : 4 * q + 4, :])
+        t2w = overlay.tile([P, TF], U32, name="t2w", offset=4 * TF, align_bytes=64)
+        nc.sync.dma_start(out=t2w[:].bitcast(I32), in_=tab2_words[0].rearrange("p t i -> p (t i)").bitcast(I32))
+        load_scale_rows(nc.sync, lambda q: w2s_raw[32 * q : 32 * q + 4, :], lambda q: w2_scales[0, 4 * q : 4 * q + 4, :])
+        wgs_t = keep.tile([P, PACK, PL], F32, name="wgs_t")
+        for q in range(4):
+            nc.sync.dma_start(out=wgs_t[32 * q : 32 * q + 32], in_=wgs.rearrange("(p t) j -> p t j", t=PACK))
+        pos_t = lists.tile([P, PL // 16], U16, name="pos_t")
+        nc.sync.dma_start(pos_t[:], pos1)
+        w3_raw.append(load_weight(ring_raw("w3_raw1"), w3, 0, group_cols(1)))
+        offs_t = lists.tile([P, S // 16], U16, name="offs_t")
+        nc.sync.dma_start(offs_t[:], offs)
+        gain_t = keep.tile([P, groups, PACK], F32, name="gain_t")
+        nc.sync.dma_start(out=gain_t[:], in_=gain.rearrange("(b p t) -> p b t", b=groups, t=PACK))
+        t1w = []
+        w1_raw = {}
+        for a in range(K // KP):
+            words = ring.tile([P, T], U32, name="t1w%d" % a, tag="big%d" % a, bufs=1, align_bytes=64)
+            nc.sync.dma_start(out=words[:].bitcast(I32), in_=tab_words[a].rearrange("p t i -> p (t i)").bitcast(I32))
+            t1w.append(words)
+            w1_raw[a, 0] = load_weight(ring_raw("w1_raw%d0" % a), w1, a, group_cols(0))
+            if a == 0:
+                load_scale_rows(nc.sync, lambda q: t1s[32 * q : 32 * q + 8, :], lambda q: tab_scales[:, 4 * q : 4 * q + 4, :])
+
+        w2w = keep.tile([P, 2 * H], U8, name="w2w", align_bytes=64)
+        nc.vector.tensor_copy(
+            out=w2w[:].rearrange("p (t c e) -> p t c e", t=PACK, e=2),
+            in_=w2w_raw[:].rearrange("p (c t e) -> p t c e", t=PACK, e=2),
+        )
+        def dealt_views(grouped, raw):
+            return (
+                grouped[:].rearrange("p (t m j) -> p m j t", t=PACK, j=PACK),
+                raw[:].rearrange("p j (m t) -> p m j t", t=PACK),
+            )
+
+        def woven(flat):
+            return flat.rearrange("p (c i t) -> p c t i", i=4, t=PACK)
+
+        def planar(planes):
+            return planes.rearrange("p t (c i) -> p c t i", i=4)
+
+        def group_tile(name):
+            return ring.tile([P, PACK * BANK], BF16, name=name, tag="grp", bufs=2, align_bytes=64)
+
+        w3q = []
+        for b in range(groups):
+            grouped = group_tile("w3_grp%d" % b)
+            dst, src = dealt_views(grouped, w3_raw[b])
+            nc.scalar.copy(out=dst, in_=src)
+            w3q.append(quantize("w3q%d" % b, grouped[:]))
+
+        v2w = keep.tile([P, PL], U32, name="v2w", align_bytes=64)
+        v2s = keep.tile([P, PL], U8, name="v2s", align_bytes=64)
+        nc.vector.tensor_copy(v2s[:], t2s[:].indirect(offs2_t[:]))
+        nc.vector.tensor_copy(v2w[:], t2w[:].indirect(offs2_t[:]))
+        w2s = keep.tile([P, H], U8, name="w2s", align_bytes=64)
+        nc.vector.tensor_copy(
+            out=w2s[:].rearrange("p (t c) -> p t c", t=PACK),
+            in_=w2s_raw[:].rearrange("p (c t) -> p t c", t=PACK),
+        )
+
+        def film_product(i, of_w2, tag):
+            b, t = divmod(i, PACK)
+            if of_w2:
+                c0 = (t * groups + b) * P
+                codes, plane = w2w[:, 2 * c0 : 2 * (c0 + P)].bitcast(FP4X4), w2s[:, c0 : c0 + P]
+            else:
+                words, scales = w3q[b]
+                codes, plane = words[:, t * P : (t + 1) * P].bitcast(FP8X4), scales[:, t * P : (t + 1) * P]
+            bank = psum.tile([P, BANK], F32, name="%s%d" % (tag, i), tag=tag, bufs=2)
+            nc.tensor.matmul_mx(
+                out=bank[:], lhsT=codes, lhsT_scale=plane,
+                rhs=v2w[:].bitcast(FP8X4), rhs_scale=v2s[:], start=True, stop=True,
+            )
+            return bank
+
+        b2_sb = []
+        for i in range(groups * PACK):
+            bank = film_product(i, i >= PACK, "b2")
+            staged = ring.tile([P, BANK], F32, name="b2_sb%d" % i, tag="row", bufs=8)
+            nc.scalar.copy(out=staged[:], in_=bank[:])
+            b2_sb.append(staged)
+
+        def place(i, product):
+            bank = film_product(i, i < PACK, "b3")
+            nc.vector.tensor_tensor(product, bank[:], b2_sb[i][:], ALU.mult)
+            nc.vector.tensor_tensor(pages[i][:].indirect(pos_t[:]), product, wgs_t[:, i % PACK, :], ALU.mult)
+
+        for i in range(PACK):
+            page = overlay.tile([P, S], F32, name="page%d" % (PACK + i), offset=4 * S * i, align_bytes=64)
+            nc.gpsimd.memset(page[:], 0.0)
+            pages.append(page)
+        place(0, b2_sb[0][:])
+        place(1, b2_sb[1][:])
+
+        for a in range(K // KP):
+            w1_raw[a, 1] = load_weight(ring_raw("w1_raw%d1" % a), w1, a, group_cols(1))
+        vw = [keep.tile([P, S], U32, name="vw%d" % a, align_bytes=64) for a in range(K // KP)]
+        vs = keep.tile([P, S], U8, name="vs", align_bytes=64)
+        w1_grp, w1q = [], {}
+        for n, (a, b) in enumerate(((0, 0), (1, 0), (0, 1), (1, 1))):
+            if b == 0:
+                nc.vector.tensor_copy(vw[a][:], t1w[a][:].indirect(offs_t[:]))
+            if n == 1:
+                nc.vector.tensor_copy(vs[:], t1s[:].indirect(offs_t[:]))
+            grouped = keep.tile([P, PACK * BANK], BF16, name="w1_grp%d" % n, align_bytes=64)
+            dst, src = dealt_views(grouped, w1_raw[a, b])
+            nc.scalar.copy(out=dst, in_=src)
+            w1q[a, b] = quantize("w1q%d" % n, grouped[:])
+            w1_grp.append(grouped)
+            place(2 + n, grouped[:].bitcast(F32)[:, 0:BANK])
+        place(6, b2_sb[6][:])
+        place(7, b2_sb[7][:])
+
+        w5_raw = [load_weight(ring_raw("w5_raw%d" % a), w5, a, slice(0, N)) for a in range(groups)]
+        w4w = keep.tile([P, groups, 2 * N], U8, name="w4w", align_bytes=64)
+        nc.sync.dma_start(out=w4w[:].bitcast(I32), in_=w4_words.rearrange("a p c -> p a c").bitcast(I32))
+        load_scale_rows(
+            nc.sync, lambda q: w4s[32 * q : 32 * q + 4], lambda q: w4_scales[:, 4 * q : 4 * q + 4, :].rearrange("a r n -> r a n")
+        )
+        gm_t = []
+        for h in range(halves):
+            tile = ring.tile([P, groups, PACK, BANK], F32, name="gm%d" % h, tag="big%d" % h, bufs=1, align_bytes=64)
+            for b in range(groups):
+                nc.sync.dma_start(
+                    out=tile[:, b],
+                    in_=gm[group_cols(b), h * BANK : (h + 1) * BANK].rearrange("(p t) j -> p t j", t=PACK),
+                )
+            gm_t.append(tile)
+
+        scratch2 = late.tile([P, 2, PACK, BANK], F32, name="scratch", offset=0, align_bytes=64)
+        feat = {}
+        for h in range(halves):
+            for b in range(groups):
+                scratch = scratch2[:, b]
+                cols = slice(h * BANK, (h + 1) * BANK)
+                e = keep.tile([P, PACK, BANK], F32, name="feat%d%d" % (b, h))
+                for t in range(PACK):
+                    bank = psum.tile([P, BANK], F32, name="a%d%d%d" % (b, h, t), tag="acc", bufs=4)
+                    for a in range(K // KP):
+                        words, scales = w1q[a, b]
+                        nc.tensor.matmul_mx(
+                            out=bank[:], lhsT=words[:, t * P : (t + 1) * P].bitcast(FP8X4),
+                            lhsT_scale=scales[:, t * P : (t + 1) * P],
+                            rhs=vw[a][:, cols].bitcast(FP8X4), rhs_scale=vs[4 * a : P, cols],
+                            start=(a == 0), stop=(a == K // KP - 1),
+                        )
+                    nc.scalar.activation(out=scratch[:, t, :], in_=bank[:], func=ACT.Tanh)
+                    if t % 2 == 1:
+                        nc.scalar.activation(out=e[:, t - 1 : t + 1, :], in_=scratch[:, t - 1 : t + 1, :], func=ACT.Exp)
+                feat[b, h] = e
+
+        w5q = []
+        for a in range(groups):
+            grouped = group_tile("w5_grp%d" % a)
+            nc.scalar.copy(out=woven(grouped[:]), in_=planar(w5_raw[a][:]))
+            w5q.append(quantize("w5q%d" % a, grouped[:]))
+
+        unit_bytes = 2 * PACK * BANK
+        za_q, zg_q, za_t = {}, {}, {}
+
+        def size_part(h, b):
+            z = feat[b, h]
+            cols = slice(h * BANK, (h + 1) * BANK)
+            for t in range(PACK):
+                nc.vector.scalar_tensor_tensor(
+                    out=z[:, t, :], in0=z[:, t, :], scalar=gain_t[:, b, t : t + 1],
+                    in1=pages[b * PACK + t][:, cols], op0=ALU.mult, op1=ALU.subtract,
+                )
+            za = late.tile([P, PACK * BANK], BF16, name="za%d%d" % (h, b), offset=(h * groups + b) * unit_bytes, align_bytes=64)
+            nc.scalar.activation(out=woven(za[:]), in_=planar(z[:]), func=ACT.Abs)
+            za_q[h, b] = quantize("zaq%d%d" % (h, b), za[:])
+
+        def signed_part(h, b):
+            if h == 0:
+                zg = w1_grp[b]
+            else:
+                zg = late.tile([P, PACK * BANK], BF16, name="zg%d" % b, offset=(2 * b + 1) * unit_bytes, align_bytes=64)
+            nc.vector.tensor_tensor(woven(zg[:]), planar(feat[b, h][:]), planar(gm_t[h][:, b]), ALU.mult)
+            zg_q[h, b] = quantize("zgq%d%d" % (h, b), zg[:])
+
+        for h in range(halves):
+            cols = slice(h * BANK, (h + 1) * BANK)
+            tags = ["acc"] * 4 if h == 1 else ["b2", "b2", "b3", "b3"]
+            banks = [
+                psum.tile([P, BANK], F32, name="o%d%d" % (h, n), tag=tags[n], bufs=4 if h == 1 else 2)
+                for n in range(N // P)
+            ]
+            for b in range(groups):
+                size_part(h, b)
+                signed_part(h, b)
+            order = ((1, 0), (0, 0), (0, 1), (1, 1)) if h == 0 else ((1, 0), (0, 0), (1, 1), (0, 1))
+            for k, (is_size, b) in enumerate(order):
+                mov_w, mov_s = za_q[h, b] if is_size else zg_q[h, b]
+                for n in range(N // P):
+                    if is_size:
+                        codes = w5q[b][0][:, n * P : (n + 1) * P].bitcast(FP8X4)
+                        plane = w5q[b][1][:, n * P : (n + 1) * P]
+                    else:
+                        codes = w4w[:, b, 2 * n * P : 2 * (n + 1) * P].bitcast(FP4X4)
+                        plane = w4s[:, b, n * P : (n + 1) * P]
+                    nc.tensor.matmul_mx(
+                        out=banks[n][:], lhsT=codes, lhsT_scale=plane,
+                        rhs=mov_w[:].bitcast(FP8X4), rhs_scale=mov_s[:],
+                        start=(k == 0), stop=(k == len(order) - 1),
+                    )
+            for n in range(N // P):
+                staged = ring.tile([P, BANK], F32, name="out%d%d" % (h, n), tag="row", bufs=8)
+                if h == halves - 1 and n % 2 == 1:
+                    nc.vector.tensor_copy(out=staged[:], in_=banks[n][:])
+                else:
+                    nc.scalar.copy(out=staged[:], in_=banks[n][:])
+                nc.sync.dma_start(out=out[n * P : (n + 1) * P, cols], in_=staged[:])

@@ -35,11 +35,15 @@ def tile_list_crash_injury_scores_kernel(
         keep = ctx.enter_context(tc.tile_pool(name="keep", bufs=1))
         ring = ctx.enter_context(tc.tile_pool(name="ring", bufs=1))
         overlay = ctx.enter_context(tc.tile_pool(name="overlay", bufs=1))
+        early = ctx.enter_context(tc.tile_pool(name="early", bufs=1))
         late = ctx.enter_context(tc.tile_pool(name="late", bufs=1))
         psum = ctx.enter_context(tc.psum_pool(name="psum", bufs=1))
 
+        def bank_tile(name, bank):
+            return psum.tile([P, BANK], F32, name=name, offset=4 * BANK * bank)
+
         def raw_tile(name, shape, dtype):
-            return ring.tile(shape, dtype, name=name, tag="raw", bufs=3, align_bytes=64)
+            return ring.tile(shape, dtype, name=name, tag="raw", bufs=4, align_bytes=64)
 
         def code_tiles(name):
             words = ring.tile([P, BANK], U32, name=name + "_w", tag="words", bufs=8, align_bytes=64)
@@ -59,10 +63,10 @@ def tile_list_crash_injury_scores_kernel(
         w2s_raw = keep.tile([P, H], U8, name="w2s_raw", align_bytes=64)
         t1s = keep.tile([P, T], U8, name="t1s", align_bytes=64)
         w4s = keep.tile([P, groups, N], U8, name="w4s", align_bytes=64)
-        nc.gpsimd.memset(t2s[:].bitcast(I32), 0)
-        nc.gpsimd.memset(w2s_raw[:].bitcast(I32), 0)
+        nc.vector.memset(t2s[:].bitcast(I32), 0)
+        nc.vector.memset(w2s_raw[:].bitcast(I32), 0)
         nc.vector.memset(t1s[:].bitcast(I32), 0)
-        nc.gpsimd.memset(w4s[:].rearrange("p a n -> p (a n)").bitcast(I32), 0)
+        nc.vector.memset(w4s[:].rearrange("p a n -> p (a n)").bitcast(I32), 0)
         pages = [keep.tile([P, S], F32, name="page%d" % i) for i in range(PACK)]
         for i in range(PACK):
             nc.vector.memset(pages[i][:], 0.0)
@@ -87,25 +91,29 @@ def tile_list_crash_injury_scores_kernel(
         t2w = overlay.tile([P, TF], U32, name="t2w", offset=4 * TF, align_bytes=64)
         nc.sync.dma_start(out=t2w[:].bitcast(I32), in_=tab2_words[0].rearrange("p t i -> p (t i)").bitcast(I32))
         load_scale_rows(nc.sync, lambda q: w2s_raw[32 * q : 32 * q + 4, :], lambda q: w2_scales[0, 4 * q : 4 * q + 4, :])
-        wgs_t = keep.tile([P, PACK, PL], F32, name="wgs_t")
-        for q in range(4):
-            nc.sync.dma_start(out=wgs_t[32 * q : 32 * q + 32], in_=wgs.rearrange("(p t) j -> p t j", t=PACK))
+
         pos_t = lists.tile([P, PL // 16], U16, name="pos_t")
         nc.sync.dma_start(pos_t[:], pos1)
-        w3_raw.append(load_weight(ring_raw("w3_raw1"), w3, 0, group_cols(1)))
-        offs_t = lists.tile([P, S // 16], U16, name="offs_t")
-        nc.sync.dma_start(offs_t[:], offs)
-        gain_t = keep.tile([P, groups, PACK], F32, name="gain_t")
-        nc.sync.dma_start(out=gain_t[:], in_=gain.rearrange("(b p t) -> p b t", b=groups, t=PACK))
-        t1w = []
-        w1_raw = {}
-        for a in range(K // KP):
+
+        def load_wgs(pair):
+            tile = keep.tile([P, 2, PL], F32, name="wgs%d" % pair)
+            rows = wgs.rearrange("(p t) j -> p t j", t=PACK)[:, 2 * pair : 2 * pair + 2, :]
+            for q in (0, 2, 1, 3):
+                nc.sync.dma_start(out=tile[32 * q : 32 * q + 32], in_=rows)
+            return tile
+
+        def load_table(a):
             words = ring.tile([P, T], U32, name="t1w%d" % a, tag="big%d" % a, bufs=1, align_bytes=64)
             nc.sync.dma_start(out=words[:].bitcast(I32), in_=tab_words[a].rearrange("p t i -> p (t i)").bitcast(I32))
-            t1w.append(words)
-            w1_raw[a, 0] = load_weight(ring_raw("w1_raw%d0" % a), w1, a, group_cols(0))
-            if a == 0:
-                load_scale_rows(nc.sync, lambda q: t1s[32 * q : 32 * q + 8, :], lambda q: tab_scales[:, 4 * q : 4 * q + 4, :])
+            return words
+
+        wgs_t = [load_wgs(0)]
+        offs_t = lists.tile([P, S // 16], U16, name="offs_t")
+        nc.sync.dma_start(offs_t[:], offs)
+        t1w = [load_table(0)]
+        wgs_t.append(load_wgs(1))
+        t1w.append(load_table(1))
+        load_scale_rows(nc.sync, lambda q: t1s[32 * q : 32 * q + 8, :], lambda q: tab_scales[:, 4 * q : 4 * q + 4, :])
 
         w2w = keep.tile([P, 2 * H], U8, name="w2w", align_bytes=64)
         nc.vector.tensor_copy(
@@ -125,26 +133,24 @@ def tile_list_crash_injury_scores_kernel(
             return planes.rearrange("p t (c i) -> p c t i", i=4)
 
         def group_tile(name):
-            return ring.tile([P, PACK * BANK], BF16, name=name, tag="grp", bufs=2, align_bytes=64)
-
-        w3q = []
-        for b in range(groups):
-            grouped = group_tile("w3_grp%d" % b)
-            dst, src = dealt_views(grouped, w3_raw[b])
-            nc.scalar.copy(out=dst, in_=src)
-            w3q.append(quantize("w3q%d" % b, grouped[:]))
+            return ring.tile([P, PACK * BANK], BF16, name=name, tag="grp", bufs=7, align_bytes=64)
 
         v2w = keep.tile([P, PL], U32, name="v2w", align_bytes=64)
         v2s = keep.tile([P, PL], U8, name="v2s", align_bytes=64)
         nc.vector.tensor_copy(v2s[:], t2s[:].indirect(offs2_t[:]))
-        nc.vector.tensor_copy(v2w[:], t2w[:].indirect(offs2_t[:]))
+        grouped = group_tile("w3_grp0")
+        dst, src = dealt_views(grouped, w3_raw[0])
+        nc.scalar.copy(out=dst[:, 0 : P // 2], in_=src[:, 0 : P // 2])
+        nc.vector.tensor_copy(out=dst[:, P // 2 : P], in_=src[:, P // 2 : P])
+        w3q = [quantize("w3q0", grouped[:])]
         w2s = keep.tile([P, H], U8, name="w2s", align_bytes=64)
         nc.vector.tensor_copy(
             out=w2s[:].rearrange("p (t c) -> p t c", t=PACK),
             in_=w2s_raw[:].rearrange("p (c t) -> p t c", t=PACK),
         )
+        nc.vector.tensor_copy(v2w[:], t2w[:].indirect(offs2_t[:]))
 
-        def film_product(i, of_w2, tag):
+        def film_product(i, of_w2, at):
             b, t = divmod(i, PACK)
             if of_w2:
                 c0 = (t * groups + b) * P
@@ -152,7 +158,7 @@ def tile_list_crash_injury_scores_kernel(
             else:
                 words, scales = w3q[b]
                 codes, plane = words[:, t * P : (t + 1) * P].bitcast(FP8X4), scales[:, t * P : (t + 1) * P]
-            bank = psum.tile([P, BANK], F32, name="%s%d" % (tag, i), tag=tag, bufs=2)
+            bank = bank_tile("film%d_%d" % (2 if of_w2 else 3, i), at)
             nc.tensor.matmul_mx(
                 out=bank[:], lhsT=codes, lhsT_scale=plane,
                 rhs=v2w[:].bitcast(FP8X4), rhs_scale=v2s[:], start=True, stop=True,
@@ -160,44 +166,74 @@ def tile_list_crash_injury_scores_kernel(
             return bank
 
         b2_sb = []
-        for i in range(groups * PACK):
-            bank = film_product(i, i >= PACK, "b2")
-            staged = ring.tile([P, BANK], F32, name="b2_sb%d" % i, tag="row", bufs=8)
+
+        def stage_product(i):
+            bank = film_product(i, i >= PACK, 2 * i if i < 2 else 1 + 2 * (i % 2))
+            if i < PACK:
+                staged = early.tile([P, BANK], F32, name="b2_sb%d" % i, offset=4 * BANK * i, align_bytes=64)
+            else:
+                staged = ring.tile([P, BANK], F32, name="b2_sb%d" % i, tag="row", bufs=4)
             nc.scalar.copy(out=staged[:], in_=bank[:])
             b2_sb.append(staged)
 
-        def place(i, product):
-            bank = film_product(i, i < PACK, "b3")
-            nc.vector.tensor_tensor(product, bank[:], b2_sb[i][:], ALU.mult)
-            nc.vector.tensor_tensor(pages[i][:].indirect(pos_t[:]), product, wgs_t[:, i % PACK, :], ALU.mult)
+        def home(i):
+            return b2_sb[i % 2] if i < PACK else b2_sb[i]
+
+        def multiply(i):
+            bank = film_product(i, i < PACK, (1, 3, 0, 2, 0, 2, 1, 3)[i])
+            nc.vector.tensor_tensor(home(i)[:], bank[:], b2_sb[i][:], ALU.mult)
+
+        def scatter(i):
+            pair, t = divmod(i % PACK, 2)
+            nc.vector.tensor_tensor(pages[i][:].indirect(pos_t[:]), home(i)[:], wgs_t[pair][:, t, :], ALU.mult)
+
+        def place_pair(first):
+            multiply(first)
+            multiply(first + 1)
+            scatter(first)
+            scatter(first + 1)
 
         for i in range(PACK):
             page = overlay.tile([P, S], F32, name="page%d" % (PACK + i), offset=4 * S * i, align_bytes=64)
             nc.gpsimd.memset(page[:], 0.0)
             pages.append(page)
-        place(0, b2_sb[0][:])
-        place(1, b2_sb[1][:])
+        for first in (0, 2):
+            stage_product(first)
+            stage_product(first + 1)
+            place_pair(first)
+        for i in range(PACK, groups * PACK):
+            stage_product(i)
 
-        for a in range(K // KP):
-            w1_raw[a, 1] = load_weight(ring_raw("w1_raw%d1" % a), w1, a, group_cols(1))
-        vw = [keep.tile([P, S], U32, name="vw%d" % a, align_bytes=64) for a in range(K // KP)]
-        vs = keep.tile([P, S], U8, name="vs", align_bytes=64)
-        w1_grp, w1q = [], {}
-        for n, (a, b) in enumerate(((0, 0), (1, 0), (0, 1), (1, 1))):
-            if b == 0:
-                nc.vector.tensor_copy(vw[a][:], t1w[a][:].indirect(offs_t[:]))
-            if n == 1:
-                nc.vector.tensor_copy(vs[:], t1s[:].indirect(offs_t[:]))
-            grouped = keep.tile([P, PACK * BANK], BF16, name="w1_grp%d" % n, align_bytes=64)
-            dst, src = dealt_views(grouped, w1_raw[a, b])
+        vw = [early.tile([P, S], U32, name="vw%d" % a, offset=(5 * S, S)[a], align_bytes=64) for a in range(K // KP)]
+        vs = early.tile([P, S], U8, name="vs", offset=0, align_bytes=64)
+        nc.vector.tensor_copy(vw[0][:], t1w[0][:].indirect(offs_t[:]))
+        nc.vector.tensor_copy(vs[:], t1s[:].indirect(offs_t[:]))
+        nc.vector.tensor_copy(vw[1][:], t1w[1][:].indirect(offs_t[:]))
+
+        def dealt_weight(name, w, a, b, raw):
+            load_weight(raw, w, a, group_cols(b))
+            grouped = group_tile(name + "_grp")
+            dst, src = dealt_views(grouped, raw)
             nc.scalar.copy(out=dst, in_=src)
-            w1q[a, b] = quantize("w1q%d" % n, grouped[:])
-            w1_grp.append(grouped)
-            place(2 + n, grouped[:].bitcast(F32)[:, 0:BANK])
-        place(6, b2_sb[6][:])
-        place(7, b2_sb[7][:])
+            return quantize(name + "_q", grouped[:])
 
-        w5_raw = [load_weight(ring_raw("w5_raw%d" % a), w5, a, slice(0, N)) for a in range(groups)]
+        w1q = {}
+        for b in range(groups):
+            for a in range(K // KP):
+                w1q[a, b] = dealt_weight("w1_%d%d" % (a, b), w1, a, b, ring_raw("w1_raw%d%d" % (a, b)))
+        w3q.append(dealt_weight("w3_1", w3, 0, 1, ring_raw("w3_raw1")))
+        w5q = []
+        for a in range(groups):
+            raw = late.tile([P, PACK, BANK], F32, name="w5_raw%d" % a, offset=4 * PACK * BANK * a, align_bytes=64)
+            load_weight(raw, w5, a, slice(0, N))
+            grouped = group_tile("w5_grp%d" % a)
+            nc.scalar.copy(out=woven(grouped[:]), in_=planar(raw[:]))
+            w5q.append(quantize("w5q%d" % a, grouped[:]))
+        place_pair(4)
+        place_pair(6)
+
+        gain_t = keep.tile([P, groups, PACK], F32, name="gain_t")
+        nc.sync.dma_start(out=gain_t[:], in_=gain.rearrange("(b p t) -> p b t", b=groups, t=PACK))
         w4w = keep.tile([P, groups, 2 * N], U8, name="w4w", align_bytes=64)
         nc.sync.dma_start(out=w4w[:].bitcast(I32), in_=w4_words.rearrange("a p c -> p a c").bitcast(I32))
         load_scale_rows(
@@ -221,7 +257,7 @@ def tile_list_crash_injury_scores_kernel(
                 cols = slice(h * BANK, (h + 1) * BANK)
                 e = keep.tile([P, PACK, BANK], F32, name="feat%d%d" % (b, h))
                 for t in range(PACK):
-                    bank = psum.tile([P, BANK], F32, name="a%d%d%d" % (b, h, t), tag="acc", bufs=4)
+                    bank = bank_tile("a%d%d%d" % (b, h, t), PACK + t)
                     for a in range(K // KP):
                         words, scales = w1q[a, b]
                         nc.tensor.matmul_mx(
@@ -234,12 +270,6 @@ def tile_list_crash_injury_scores_kernel(
                     if t % 2 == 1:
                         nc.scalar.activation(out=e[:, t - 1 : t + 1, :], in_=scratch[:, t - 1 : t + 1, :], func=ACT.Exp)
                 feat[b, h] = e
-
-        w5q = []
-        for a in range(groups):
-            grouped = group_tile("w5_grp%d" % a)
-            nc.scalar.copy(out=woven(grouped[:]), in_=planar(w5_raw[a][:]))
-            w5q.append(quantize("w5q%d" % a, grouped[:]))
 
         unit_bytes = 2 * PACK * BANK
         za_q, zg_q, za_t = {}, {}, {}
@@ -258,39 +288,53 @@ def tile_list_crash_injury_scores_kernel(
 
         def signed_part(h, b):
             if h == 0:
-                zg = w1_grp[b]
+                zg = group_tile("zg0%d" % b)
             else:
                 zg = late.tile([P, PACK * BANK], BF16, name="zg%d" % b, offset=(2 * b + 1) * unit_bytes, align_bytes=64)
-            nc.vector.tensor_tensor(woven(zg[:]), planar(feat[b, h][:]), planar(gm_t[h][:, b]), ALU.mult)
-            zg_q[h, b] = quantize("zgq%d%d" % (h, b), zg[:])
+            words, scales = code_tiles("zgq%d%d" % (h, b))
+            parts = 2 if (h, b) == (halves - 1, groups - 1) else 1
+            width = BANK // parts
+            for k in range(parts):
+                cols = slice(k * width, (k + 1) * width)
+                nc.vector.tensor_tensor(
+                    woven(zg[:, PACK * k * width : PACK * (k + 1) * width]),
+                    planar(feat[b, h][:, :, cols]), planar(gm_t[h][:, b, :, cols]), ALU.mult,
+                )
+            for k in range(parts):
+                cols = slice(k * width, (k + 1) * width)
+                nc.vector.quantize_mx(
+                    out=words[:, cols].bitcast(FP8X4), scales=scales[:, cols],
+                    in_=zg[:, PACK * k * width : PACK * (k + 1) * width],
+                )
+            zg_q[h, b] = words, scales
 
         for h in range(halves):
             cols = slice(h * BANK, (h + 1) * BANK)
-            tags = ["acc"] * 4 if h == 1 else ["b2", "b2", "b3", "b3"]
-            banks = [
-                psum.tile([P, BANK], F32, name="o%d%d" % (h, n), tag=tags[n], bufs=4 if h == 1 else 2)
-                for n in range(N // P)
-            ]
+            banks = [bank_tile("o%d%d" % (h, n), (1 - h) * PACK + n) for n in range(N // P)]
             for b in range(groups):
                 size_part(h, b)
                 signed_part(h, b)
-            order = ((1, 0), (0, 0), (0, 1), (1, 1)) if h == 0 else ((1, 0), (0, 0), (1, 1), (0, 1))
+            order = ((0, 0), (0, 1), (1, 0), (1, 1)) if h == 0 else ((0, 0), (1, 0), (1, 1), (0, 1))
             for k, (is_size, b) in enumerate(order):
                 mov_w, mov_s = za_q[h, b] if is_size else zg_q[h, b]
-                for n in range(N // P):
-                    if is_size:
-                        codes = w5q[b][0][:, n * P : (n + 1) * P].bitcast(FP8X4)
-                        plane = w5q[b][1][:, n * P : (n + 1) * P]
-                    else:
-                        codes = w4w[:, b, 2 * n * P : 2 * (n + 1) * P].bitcast(FP4X4)
-                        plane = w4s[:, b, n * P : (n + 1) * P]
-                    nc.tensor.matmul_mx(
-                        out=banks[n][:], lhsT=codes, lhsT_scale=plane,
-                        rhs=mov_w[:].bitcast(FP8X4), rhs_scale=mov_s[:],
-                        start=(k == 0), stop=(k == len(order) - 1),
-                    )
+                last = k == len(order) - 1
+                spans = [[(0, P), (P, 2 * P)], [(2 * P, 3 * P), (3 * P, BANK)]] if last and h == halves - 1 else [[(0, BANK)]]
+                for part in spans:
+                    for n in range(N // P):
+                        if is_size:
+                            codes = w5q[b][0][:, n * P : (n + 1) * P].bitcast(FP8X4)
+                            plane = w5q[b][1][:, n * P : (n + 1) * P]
+                        else:
+                            codes = w4w[:, b, 2 * n * P : 2 * (n + 1) * P].bitcast(FP4X4)
+                            plane = w4s[:, b, n * P : (n + 1) * P]
+                        for c0, c1 in part:
+                            nc.tensor.matmul_mx(
+                                out=banks[n][:, c0:c1], lhsT=codes, lhsT_scale=plane,
+                                rhs=mov_w[:, c0:c1].bitcast(FP8X4), rhs_scale=mov_s[:, c0:c1],
+                                start=(k == 0), stop=(last and c1 == BANK),
+                            )
             for n in range(N // P):
-                staged = ring.tile([P, BANK], F32, name="out%d%d" % (h, n), tag="row", bufs=8)
+                staged = ring.tile([P, BANK], F32, name="out%d%d" % (h, n), tag="row", bufs=4)
                 if h == halves - 1 and n % 2 == 1:
                     nc.vector.tensor_copy(out=staged[:], in_=banks[n][:])
                 else:

from contextlib import ExitStack

import concourse.mybir as mybir

K, M, H, N, T, S, TF, PL = 1024, 512, 1024, 512, 4096, 1024, 2048, 512
FLOPS = 2 * (K * H * S + 2 * M * H * PL + 2 * H * N * S)

F32 = mybir.dt.float32
BF16 = mybir.dt.bfloat16
I32 = mybir.dt.int32
U32 = mybir.dt.uint32
U16 = mybir.dt.uint16
U8 = mybir.dt.uint8
FP8X4 = mybir.dt.float8_e4m3fn_x4
FP4X4 = mybir.dt.float4_e2m1fn_x4
ALU = mybir.AluOpType
ACT = mybir.ActivationFunctionType

P = 128
PACK = 4
KP = P * PACK
BANK = 512


def tile_list_crash_injury_scores_kernel(
    tc, tab_words, tab_scales, offs, tab2_words, tab2_scales, offs2, pos1, w1, gain,
    w2_words, w2_scales, w3, wgs, gm, w4_words, w4_scales, w5, out,
):
    nc = tc.nc
    groups = H // KP
    halves = S // BANK

    with ExitStack() as ctx:
        lists = ctx.enter_context(tc.tile_pool(name="lists", bufs=1))
        keep = ctx.enter_context(tc.tile_pool(name="keep", bufs=1))
        ring = ctx.enter_context(tc.tile_pool(name="ring", bufs=1))
        overlay = ctx.enter_context(tc.tile_pool(name="overlay", bufs=1))
        early = ctx.enter_context(tc.tile_pool(name="early", bufs=1))
        late = ctx.enter_context(tc.tile_pool(name="late", bufs=1))
        psum = ctx.enter_context(tc.psum_pool(name="psum", bufs=1))

        def bank_tile(name, bank):
            return psum.tile([P, BANK], F32, name=name, offset=4 * BANK * bank)

        def raw_tile(name, shape, dtype):
            return ring.tile(shape, dtype, name=name, tag="raw", bufs=4, align_bytes=64)

        def code_tiles(name):
            words = ring.tile([P, BANK], U32, name=name + "_w", tag="words", bufs=8, align_bytes=64)
            scales = ring.tile([P, BANK], U8, name=name + "_s", tag="scales", bufs=8, align_bytes=64)
            return words, scales

        def quantize(name, grouped):
            words, scales = code_tiles(name)
            nc.vector.quantize_mx(out=words[:].bitcast(FP8X4), scales=scales[:], in_=grouped)
            return words, scales

        def load_scale_rows(queue, tile, rows):
            for q in range(4):
                queue.dma_start(out=tile(q).bitcast(I32), in_=rows(q).bitcast(I32))

        t2s = keep.tile([P, TF], U8, name="t2s", align_bytes=64)
        w2s_raw = keep.tile([P, H], U8, name="w2s_raw", align_bytes=64)
        t1s = keep.tile([P, T], U8, name="t1s", align_bytes=64)
        w4s = keep.tile([P, groups, N], U8, name="w4s", align_bytes=64)
        nc.vector.memset(t2s[:].bitcast(I32), 0)
        nc.vector.memset(w2s_raw[:].bitcast(I32), 0)
        nc.vector.memset(t1s[:].bitcast(I32), 0)
        nc.vector.memset(w4s[:].rearrange("p a n -> p (a n)").bitcast(I32), 0)
        pages = [keep.tile([P, S], F32, name="page%d" % i) for i in range(PACK)]
        for i in range(PACK):
            nc.vector.memset(pages[i][:], 0.0)

        def load_weight(raw, w, a, cols):
            nc.sync.dma_start(out=raw[:], in_=w[a * KP : (a + 1) * KP, cols].rearrange("(p j) c -> p j c", j=PACK))
            return raw

        def ring_raw(name):
            return raw_tile(name, [P, PACK, BANK], F32)

        def group_cols(b):
            return slice(b * KP, (b + 1) * KP)

        offs2_t = lists.tile([P, PL // 16], U16, name="offs2_t")
        nc.sync.dma_start(offs2_t[:], offs2)
        w2w_raw = keep.tile([P, 2 * H], U8, name="w2w_raw", align_bytes=64)
        nc.sync.dma_start(out=w2w_raw[:].bitcast(I32), in_=w2_words[0].bitcast(I32))
        first_raw = overlay.tile([P, PACK, BANK], F32, name="w3_raw0", offset=0, align_bytes=64)
        w3_raw = [load_weight(first_raw, w3, 0, group_cols(0))]
        load_scale_rows(nc.sync, lambda q: t2s[32 * q : 32 * q + 4, :], lambda q: tab2_scales[0, 4 * q : 4 * q + 4, :])
        t2w = overlay.tile([P, TF], U32, name="t2w", offset=4 * TF, align_bytes=64)
        nc.sync.dma_start(out=t2w[:].bitcast(I32), in_=tab2_words[0].rearrange("p t i -> p (t i)").bitcast(I32))
        load_scale_rows(nc.sync, lambda q: w2s_raw[32 * q : 32 * q + 4, :], lambda q: w2_scales[0, 4 * q : 4 * q + 4, :])

        pos_t = lists.tile([P, PL // 16], U16, name="pos_t")
        nc.sync.dma_start(pos_t[:], pos1)

        def load_wgs(pair):
            tile = keep.tile([P, 2, PL], F32, name="wgs%d" % pair)
            rows = wgs.rearrange("(p t) j -> p t j", t=PACK)[:, 2 * pair : 2 * pair + 2, :]
            for q in (0, 2, 1, 3):
                nc.sync.dma_start(out=tile[32 * q : 32 * q + 32], in_=rows)
            return tile

        def load_table(a):
            words = ring.tile([P, T], U32, name="t1w%d" % a, tag="big%d" % a, bufs=1, align_bytes=64)
            nc.sync.dma_start(out=words[:].bitcast(I32), in_=tab_words[a].rearrange("p t i -> p (t i)").bitcast(I32))
            return words

        wgs_t = [load_wgs(0)]
        offs_t = lists.tile([P, S // 16], U16, name="offs_t")
        nc.sync.dma_start(offs_t[:], offs)
        t1w = [load_table(0)]
        wgs_t.append(load_wgs(1))
        t1w.append(load_table(1))
        load_scale_rows(nc.sync, lambda q: t1s[32 * q : 32 * q + 8, :], lambda q: tab_scales[:, 4 * q : 4 * q + 4, :])

        w2w = keep.tile([P, 2 * H], U8, name="w2w", align_bytes=64)
        nc.vector.tensor_copy(
            out=w2w[:].rearrange("p (t c e) -> p t c e", t=PACK, e=2),
            in_=w2w_raw[:].rearrange("p (c t e) -> p t c e", t=PACK, e=2),
        )
        def dealt_views(grouped, raw):
            return (
                grouped[:].rearrange("p (t m j) -> p m j t", t=PACK, j=PACK),
                raw[:].rearrange("p j (m t) -> p m j t", t=PACK),
            )

        def woven(flat):
            return flat.rearrange("p (c i t) -> p c t i", i=4, t=PACK)

        def planar(planes):
            return planes.rearrange("p t (c i) -> p c t i", i=4)

        def group_tile(name):
            return ring.tile([P, PACK * BANK], BF16, name=name, tag="grp", bufs=7, align_bytes=64)

        v2w = keep.tile([P, PL], U32, name="v2w", align_bytes=64)
        v2s = keep.tile([P, PL], U8, name="v2s", align_bytes=64)
        nc.vector.tensor_copy(v2s[:], t2s[:].indirect(offs2_t[:]))
        grouped = group_tile("w3_grp0")
        dst, src = dealt_views(grouped, w3_raw[0])
        nc.scalar.copy(out=dst[:, 0 : P // 2], in_=src[:, 0 : P // 2])
        nc.vector.tensor_copy(out=dst[:, P // 2 : P], in_=src[:, P // 2 : P])
        w3q = [quantize("w3q0", grouped[:])]
        w2s = keep.tile([P, H], U8, name="w2s", align_bytes=64)
        nc.vector.tensor_copy(
            out=w2s[:].rearrange("p (t c) -> p t c", t=PACK),
            in_=w2s_raw[:].rearrange("p (c t) -> p t c", t=PACK),
        )
        nc.vector.tensor_copy(v2w[:], t2w[:].indirect(offs2_t[:]))

        def film_product(i, of_w2, at):
            b, t = divmod(i, PACK)
            if of_w2:
                c0 = (t * groups + b) * P
                codes, plane = w2w[:, 2 * c0 : 2 * (c0 + P)].bitcast(FP4X4), w2s[:, c0 : c0 + P]
            else:
                words, scales = w3q[b]
                codes, plane = words[:, t * P : (t + 1) * P].bitcast(FP8X4), scales[:, t * P : (t + 1) * P]
            bank = bank_tile("film%d_%d" % (2 if of_w2 else 3, i), at)
            nc.tensor.matmul_mx(
                out=bank[:], lhsT=codes, lhsT_scale=plane,
                rhs=v2w[:].bitcast(FP8X4), rhs_scale=v2s[:], start=True, stop=True,
            )
            return bank

        b2_sb = []

        def stage_product(i):
            bank = film_product(i, i >= PACK, 2 * i if i < 2 else 1 + 2 * (i % 2))
            if i < PACK:
                staged = early.tile([P, BANK], F32, name="b2_sb%d" % i, offset=4 * BANK * i, align_bytes=64)
            else:
                staged = ring.tile([P, BANK], F32, name="b2_sb%d" % i, tag="row", bufs=4)
            nc.scalar.copy(out=staged[:], in_=bank[:])
            b2_sb.append(staged)

        def home(i):
            return b2_sb[i % 2] if i < PACK else b2_sb[i]

        def multiply(i):
            bank = film_product(i, i < PACK, (1, 3, 0, 2, 0, 2, 1, 3)[i])
            nc.vector.tensor_tensor(home(i)[:], bank[:], b2_sb[i][:], ALU.mult)

        def scatter(i):
            pair, t = divmod(i % PACK, 2)
            nc.vector.tensor_tensor(pages[i][:].indirect(pos_t[:]), home(i)[:], wgs_t[pair][:, t, :], ALU.mult)

        def place_pair(first):
            multiply(first)
            multiply(first + 1)
            scatter(first)
            scatter(first + 1)

        for i in range(PACK):
            page = overlay.tile([P, S], F32, name="page%d" % (PACK + i), offset=4 * S * i, align_bytes=64)
            nc.gpsimd.memset(page[:], 0.0)
            pages.append(page)
        for first in (0, 2):
            stage_product(first)
            stage_product(first + 1)
            place_pair(first)
        for i in range(PACK, groups * PACK):
            stage_product(i)

        vw = [early.tile([P, S], U32, name="vw%d" % a, offset=(5 * S, S)[a], align_bytes=64) for a in range(K // KP)]
        vs = early.tile([P, S], U8, name="vs", offset=0, align_bytes=64)
        nc.vector.tensor_copy(vw[0][:], t1w[0][:].indirect(offs_t[:]))
        nc.vector.tensor_copy(vs[:], t1s[:].indirect(offs_t[:]))
        nc.vector.tensor_copy(vw[1][:], t1w[1][:].indirect(offs_t[:]))

        def dealt_weight(name, w, a, b, raw):
            load_weight(raw, w, a, group_cols(b))
            grouped = group_tile(name + "_grp")
            dst, src = dealt_views(grouped, raw)
            nc.scalar.copy(out=dst, in_=src)
            return quantize(name + "_q", grouped[:])

        w1q = {}
        for b in range(groups):
            for a in range(K // KP):
                w1q[a, b] = dealt_weight("w1_%d%d" % (a, b), w1, a, b, ring_raw("w1_raw%d%d" % (a, b)))
        w3q.append(dealt_weight("w3_1", w3, 0, 1, ring_raw("w3_raw1")))
        w5q = []
        for a in range(groups):
            raw = late.tile([P, PACK, BANK], F32, name="w5_raw%d" % a, offset=4 * PACK * BANK * a, align_bytes=64)
            load_weight(raw, w5, a, slice(0, N))
            grouped = group_tile("w5_grp%d" % a)
            nc.scalar.copy(out=woven(grouped[:]), in_=planar(raw[:]))
            w5q.append(quantize("w5q%d" % a, grouped[:]))
        place_pair(4)
        place_pair(6)

        gain_t = keep.tile([P, groups, PACK], F32, name="gain_t")
        nc.sync.dma_start(out=gain_t[:], in_=gain.rearrange("(b p t) -> p b t", b=groups, t=PACK))
        w4w = keep.tile([P, groups, 2 * N], U8, name="w4w", align_bytes=64)
        nc.sync.dma_start(out=w4w[:].bitcast(I32), in_=w4_words.rearrange("a p c -> p a c").bitcast(I32))
        load_scale_rows(
            nc.sync, lambda q: w4s[32 * q : 32 * q + 4], lambda q: w4_scales[:, 4 * q : 4 * q + 4, :].rearrange("a r n -> r a n")
        )
        gm_t = []
        for h in range(halves):
            tile = ring.tile([P, groups, PACK, BANK], F32, name="gm%d" % h, tag="big%d" % h, bufs=1, align_bytes=64)
            for b in range(groups):
                nc.sync.dma_start(
                    out=tile[:, b],
                    in_=gm[group_cols(b), h * BANK : (h + 1) * BANK].rearrange("(p t) j -> p t j", t=PACK),
                )
            gm_t.append(tile)

        scratch2 = late.tile([P, 2, PACK, BANK], F32, name="scratch", offset=0, align_bytes=64)
        feat = {}
        for h in range(halves):
            for b in range(groups):
                scratch = scratch2[:, b]
                cols = slice(h * BANK, (h + 1) * BANK)
                e = keep.tile([P, PACK, BANK], F32, name="feat%d%d" % (b, h))
                for t in range(PACK):
                    bank = bank_tile("a%d%d%d" % (b, h, t), PACK + t)
                    for a in range(K // KP):
                        words, scales = w1q[a, b]
                        nc.tensor.matmul_mx(
                            out=bank[:], lhsT=words[:, t * P : (t + 1) * P].bitcast(FP8X4),
                            lhsT_scale=scales[:, t * P : (t + 1) * P],
                            rhs=vw[a][:, cols].bitcast(FP8X4), rhs_scale=vs[4 * a : P, cols],
                            start=(a == 0), stop=(a == K // KP - 1),
                        )
                    nc.scalar.activation(out=scratch[:, t, :], in_=bank[:], func=ACT.Tanh)
                    if t % 2 == 1:
                        nc.scalar.activation(out=e[:, t - 1 : t + 1, :], in_=scratch[:, t - 1 : t + 1, :], func=ACT.Exp)
                feat[b, h] = e

        unit_bytes = 2 * PACK * BANK
        za_q, zg_q, za_t = {}, {}, {}

        def size_part(h, b):
            z = feat[b, h]
            cols = slice(h * BANK, (h + 1) * BANK)
            for t in range(PACK):
                nc.vector.scalar_tensor_tensor(
                    out=z[:, t, :], in0=z[:, t, :], scalar=gain_t[:, b, t : t + 1],
                    in1=pages[b * PACK + t][:, cols], op0=ALU.mult, op1=ALU.subtract,
                )
            za = late.tile([P, PACK * BANK], BF16, name="za%d%d" % (h, b), offset=(h * groups + b) * unit_bytes, align_bytes=64)
            nc.scalar.activation(out=woven(za[:]), in_=planar(z[:]), func=ACT.Abs)
            za_q[h, b] = quantize("zaq%d%d" % (h, b), za[:])

        def signed_part(h, b):
            if h == 0:
                zg = group_tile("zg0%d" % b)
            else:
                zg = late.tile([P, PACK * BANK], BF16, name="zg%d" % b, offset=(2 * b + 1) * unit_bytes, align_bytes=64)
            words, scales = code_tiles("zgq%d%d" % (h, b))
            parts = 2 if (h, b) == (halves - 1, groups - 1) else 1
            width = BANK // parts
            for k in range(parts):
                cols = slice(k * width, (k + 1) * width)
                nc.vector.tensor_tensor(
                    woven(zg[:, PACK * k * width : PACK * (k + 1) * width]),
                    planar(feat[b, h][:, :, cols]), planar(gm_t[h][:, b, :, cols]), ALU.mult,
                )
            for k in range(parts):
                cols = slice(k * width, (k + 1) * width)
                nc.vector.quantize_mx(
                    out=words[:, cols].bitcast(FP8X4), scales=scales[:, cols],
                    in_=zg[:, PACK * k * width : PACK * (k + 1) * width],
                )
            zg_q[h, b] = words, scales

        for h in range(halves):
            cols = slice(h * BANK, (h + 1) * BANK)
            banks = [bank_tile("o%d%d" % (h, n), (1 - h) * PACK + n) for n in range(N // P)]
            for b in range(groups):
                size_part(h, b)
                signed_part(h, b)
            order = ((0, 0), (0, 1), (1, 0), (1, 1)) if h == 0 else ((0, 0), (1, 0), (1, 1), (0, 1))
            for k, (is_size, b) in enumerate(order):
                mov_w, mov_s = za_q[h, b] if is_size else zg_q[h, b]
                last = k == len(order) - 1
                spans = [[(0, P), (P, 2 * P)], [(2 * P, 3 * P), (3 * P, BANK)]] if last and h == halves - 1 else [[(0, BANK)]]
                for part in spans:
                    for n in range(N // P):
                        if is_size:
                            codes = w5q[b][0][:, n * P : (n + 1) * P].bitcast(FP8X4)
                            plane = w5q[b][1][:, n * P : (n + 1) * P]
                        else:
                            codes = w4w[:, b, 2 * n * P : 2 * (n + 1) * P].bitcast(FP4X4)
                            plane = w4s[:, b, n * P : (n + 1) * P]
                        for c0, c1 in part:
                            nc.tensor.matmul_mx(
                                out=banks[n][:, c0:c1], lhsT=codes, lhsT_scale=plane,
                                rhs=mov_w[:, c0:c1].bitcast(FP8X4), rhs_scale=mov_s[:, c0:c1],
                                start=(k == 0), stop=(last and c1 == BANK),
                            )
            for n in range(N // P):
                staged = ring.tile([P, BANK], F32, name="out%d%d" % (h, n), tag="row", bufs=4)
                if h == halves - 1 and n % 2 == 1:
                    nc.vector.tensor_copy(out=staged[:], in_=banks[n][:])
                else:
                    nc.scalar.copy(out=staged[:], in_=banks[n][:])
                nc.sync.dma_start(out=out[n * P : (n + 1) * P, cols], in_=staged[:])
